import numpy as np
CORES = [10,14,66,70,74,78,82,86,90,94,106,110]
N = 12
B, TIMES = 256, 2
def setup_inputs(rng):
    return {"x": (rng.standard_normal((N, 128, B), dtype=np.float32) * (0.5 + np.abs(rng.standard_normal((1, 1, B), dtype=np.float32))) / np.float32(np.sqrt(128 * N))), "a": (rng.standard_normal((N, 128, N * 128), dtype=np.float32) / 8)}
def setup_inputs_big(rng):
    d = setup_inputs(rng)
    for k in ("a",): d[k] = (d[k].astype(np.float32) * 1048576.0).astype(d[k].dtype)
    return d
def setup_inputs_small(rng):
    d = setup_inputs(rng)
    for k in ("a",): d[k] = (d[k].astype(np.float32) * (1 / 1048576.0)).astype(d[k].dtype)
    return d
def setup_inputs_apart(rng):
    d = setup_inputs(rng)
    f = (10.0 ** rng.permutation(np.linspace(-1.5, 1.5, N))).astype(np.float32).reshape(N, 1, 1)
    for k in ("a",): d[k] = (d[k].astype(np.float32) * f).astype(d[k].dtype)
    return d
def reference(x, a):
    X, A = x.astype(np.float64), a.astype(np.float64)
    h = X
    for _ in range(TIMES):
        h = np.stack([sum(A[r][:, 128 * j:128 * j + 128].T @ h[j] for j in range(N)) for r in range(N)])
        h = h / np.sqrt((h ** 2).sum(axis=(0, 1)))
        h = h + X
    return {"y": h.astype(np.float32)}

@@ -1,0 +1,322 @@
+from concourse.bass import DstId, RemoteDMATransfer
+from concourse.mybir import AluOpType, AxisListType, ActivationFunctionType
+
+_F = "float32"
+SCRATCH = {
+    "A": ("sbuf", [128, 3072], _F),
+    "XF": ("sbuf", [128, 256], _F),
+    "XB": ("sbuf", [128, 768], _F),
+    "UB": ("sbuf", [128, 768], _F),
+    "SQ": ("sbuf", [128, 768], _F),
+    "ACC": ("sbuf", [128, 128], _F),
+    "ONES": ("sbuf", [128, 128], _F),
+    "TWOS": ("sbuf", [128, 64], _F),
+    "E3A": ("sbuf", [128, 64], _F),
+    "E3B": ("sbuf", [128, 64], _F),
+    "E3C": ("sbuf", [128, 64], _F),
+    "Z": ("sbuf", [128, 256], _F),
+    "LO": ("sbuf", [128, 4], _F),
+    "L": ("sbuf", [128, 8], _F),
+    "SR": ("sbuf", [128, 4], _F),
+    "N1": ("sbuf", [128, 64], _F),
+    "D1": ("sbuf", [128, 64], _F),
+    "DSQ": ("sbuf", [128, 64], _F),
+    "RHO": ("sbuf", [128, 64], _F),
+    "RHR": ("sbuf", [128, 64], _F),
+    "TW": ("sbuf", [128, 128], _F),
+    "W": ("sbuf", [128, 128], _F),
+    "N2": ("sbuf", [128, 64], _F),
+    "YS": ("sbuf", [128, 128], _F),
+    "YF": ("sbuf", [128, 256], _F),
+    "PU0": ("psum", [128, 512], _F), "PU1": ("psum", [128, 512], _F),
+    "PV0": ("psum", [128, 512], _F), "PV1": ("psum", [128, 512], _F),
+    "PS": ("psum", [128, 512], _F), "PP": ("psum", [128, 512], _F),
+    "PB": ("psum", [128, 512], _F), "PT": ("psum", [128, 512], _F),
+}
+SEMAPHORES = (["m1", "m2", "e1", "e2", "xl", "xs", "L0", "L1", "pu0", "pu1", "c0", "c1", "pv0", "pv1",
+               "zs0", "zs1", "zv0", "zv1", "pp", "lo", "ps", "n1", "d1", "dsq", "eb", "et", "rho", "tw0", "tw1",
+               "w", "pq", "sr", "rhr", "pb", "n2", "d2", "t0", "t1", "y0", "y1", "ya", "st", "ls"]
+              + ["A%d%d" % (h, c) for h in range(2) for c in range(6)]
+              + ["xa%d" % c for c in range(6)] + ["ua%d" % c for c in range(6)]
+              + ["sq%d" % c for c in range(6)] + ["ac%d" % c for c in range(1, 6)])
+
+BW = 64
+PW = 2 * BW
+
+
+def _bits(mask):
+    return [i for i in range(16) if (mask >> i) & 1]
+
+
+def _mk(bits):
+    return sum(1 << i for i in bits)
+
+
+def rank_program(g, core, T, topo):
+    cores = list(T.cores)
+    chips = []
+    for c in cores:
+        if topo.chip(c) not in chips:
+            chips.append(topo.chip(c))
+    if topo.chip(core) not in chips:
+        return
+    nch = len(chips)
+    half = nch // 2
+    ci = chips.index(topo.chip(core))
+    rk = [[i for i, c in enumerate(cores) if topo.chip(c) == ch] for ch in chips]
+    for c in range(nch):
+        assert rk[c] == [2 * c, 2 * c + 1]
+    every = range(topo.CORES_PER_CHIP * topo.CHIPS)
+    on_chip = [[k for k in every if topo.chip(k) == ch] for ch in chips]
+    wk = [[k for k in on_chip[c] if all(topo.may_write(k, d) for d in cores if d != k)] for c in range(nch)]
+    for c in range(nch):
+        assert len(wk[c]) * BW == 256
+    rc = [cores[r] for r in rk[ci]]
+    idle = [k for k in on_chip[ci] if k not in wk[ci]]
+    xs_of = [[k for k in idle if topo.die(k) == topo.die(rc[h])][:2] for h in range(2)]
+
+    def S(n):
+        return T.sem[n]
+
+    def did(k):
+        rid, pid, _s = topo.addr(k)
+        return DstId(rid=rid, pnc=pid)
+
+    def src_at(cj, s):
+        q_, l = divmod(cj, half)
+        return (q_ if s < half else 1 - q_) * half + (l - s) % half
+
+    def dst_at(cj, s):
+        q_, l = divmod(cj, half)
+        return (q_ if s < half else 1 - q_) * half + (l + s) % half
+
+    def acol(h, c):
+        return 128 * 2 * nch * h + 128 * rk[c][0]
+
+    order = [src_at(ci, s) for s in range(nch)]
+    sent = [0]
+
+    def fused(trs):
+        g.remote_dma_fused([m[0] for m in trs], local_sem=S("ls"))
+        for m in trs:
+            sent[0] += m[1]
+
+    def tr(dsts_cores, mask, sem, src, dsts):
+        return (RemoteDMATransfer(dst_ids=[did(k) for k in dsts_cores], dma_engine_mask=mask, remote_sem=S(sem),
+                                  srcs=[src], dsts=dsts, alu_op=0), len(_bits(mask)))
+
+    if core in idle:
+        for h in range(2):
+            if core in xs_of[h]:
+                k = xs_of[h].index(core)
+                to = [w for w in wk[ci] if w != rc[h]]
+                mask = topo.mask(core, to[0])
+                for w in to:
+                    mask &= topo.mask(core, w)
+                g.wait_ge(S("L%d" % k), len(_bits(topo.mask(rc[h], core))))
+                for s in range(k * half, (k + 1) * half):
+                    c = order[s]
+                    ap = T.A[:, acol(h, c):acol(h, c) + 256]
+                    fused([tr(to, mask, "A%d%d" % (h, c), ap, [ap for _w in to])])
+                g.wait_ge(S("ls"), sent[0])
+        return
+
+    b = wk[ci].index(core)
+    me_h = rc.index(core) if core in rc else None
+    peers = [wk[dst_at(ci, s)][b] for s in range(1, nch)]
+    off = topo.mask(core, peers[0])
+    for k in peers:
+        off &= topo.mask(core, k)
+    n_off = len(_bits(off))
+    mates_here = [w for w in wk[ci] if w != core]
+    on = topo.mask(core, mates_here[0])
+    for k in mates_here:
+        on &= topo.mask(core, k)
+    onb = _bits(on)
+    n_on = len(onb)
+    o = PW * ci
+    own_x = T.XB[:, o:o + PW]
+    own_u = T.UB[:, o:o + PW]
+    V, Sc, Te = g.vector, g.scalar, g.tensor
+    mult, add = AluOpType.mult, AluOpType.add
+    q4 = n_on // 4
+
+    V.memset(T.ONES[:], 1.0).then_inc(S("m1"), 1)
+    V.memset(T.TWOS[:], 2.0).then_inc(S("m2"), 1)
+
+    q = ci // half
+    hw = 256 * half
+    if me_h is not None:
+        g.sync.dma_start(T.XF[:], T.x[:]).then_inc(S("xl"), 16)
+        Sc.dma_start(T.XB[:, o + BW * me_h:o + BW * me_h + BW], T.x[:, BW * b:BW * b + BW]).then_inc(S("xs"), 16)
+        a0, a1 = acol(me_h, q * half), acol(me_h, (1 - q) * half)
+        g.sync.dma_start(T.A[:, a0:a0 + hw], T.a[:, hw * q:hw * q + hw]).then_inc(S("L0"), 16)
+        Sc.dma_start(T.A[:, a1:a1 + hw], T.a[:, hw * (1 - q):hw * (1 - q) + hw]).then_inc(S("L1"), 16)
+
+    g.wait_ge(S("m1"), 1)
+    g.wait_ge(S("m2"), 1)
+    g.affine_select(T.E3A[:], T.ONES[:, 0:BW], [[-1, BW]], AluOpType.is_equal, 0.0, 0, 1).then_inc(S("e1"), 1)
+    g.affine_select(T.E3B[:], T.TWOS[:], [[-1, BW]], AluOpType.is_equal, 0.0, -BW, 1).then_inc(S("e2"), 1)
+
+    xs_total = sum(q4 for h in range(2) if rc[h] != core) + (16 if me_h is not None else 0)
+    if me_h is not None:
+        g.wait_ge(S("xl"), 16)
+        trs = []
+        for i, w in enumerate(mates_here):
+            bw_ = wk[ci].index(w)
+            trs.append(tr([w], _mk(onb[q4 * (i + 1):q4 * (i + 2)]), "xs", T.XF[:, BW * bw_:BW * bw_ + BW],
+                          [T.XB[:, o + BW * me_h:o + BW * me_h + BW]]))
+        fused(trs)
+        for k, a_ in enumerate((a0, a1)):
+            g.wait_ge(S("L%d" % k), 16)
+            x_ = xs_of[me_h][k]
+            rid, pid, _s = topo.addr(x_)
+            mk_ = topo.mask(core, x_)
+            g.remote_dma(out_ap=T.A[:, a_:a_ + hw], in_ap=T.A[:, a_:a_ + hw], remote_sem=S("L%d" % k),
+                         local_sem=S("ls"), pid=pid, routing_id=rid, dma_engine_mask=mk_)
+            sent[0] += len(_bits(mk_))
+
+    g.wait_ge(S("xs"), xs_total)
+    fused([tr(peers, off, "xa%d" % ci, own_x, [own_x for _k in peers])])
+
+    def a_wait(h, c, s):
+        if me_h == h:
+            Te.wait_ge(S("L%d" % (s // half)), 16)
+        else:
+            Te.wait_ge(S("A%d%d" % (h, c)), n_on)
+
+    def mm_pass(buf, outs, done, first):
+        for s, c in enumerate(order):
+            if s == 0:
+                first()
+            else:
+                Te.wait_ge(S("%s%d" % (done[2], c)), n_off)
+            for h in range(2):
+                if done[2] == "xa":
+                    a_wait(h, c, s)
+                for jj in range(2):
+                    ac_ = acol(h, c) + 128 * jj
+                    ins = Te.matmul(out=outs[h][:, 0:BW], lhsT=T.A[:, ac_:ac_ + 128],
+                                    rhs=buf[:, PW * c + BW * jj:PW * c + BW * jj + BW],
+                                    start=(s == 0 and jj == 0), stop=(s == nch - 1 and jj == 1))
+                    if s == nch - 1 and jj == 1:
+                        ins.then_inc(S(done[h]), 1)
+
+    mm_pass(T.XB, (T.PU0, T.PU1), ("pu0", "pu1", "xa"), lambda: Te.wait_ge(S("xs"), xs_total))
+
+    for h, pu in enumerate((T.PU0, T.PU1)):
+        V.wait_ge(S("pu%d" % h), 1)
+        V.tensor_copy(T.UB[:, o + BW * h:o + BW * h + BW], pu[:, 0:BW]).then_inc(S("c%d" % h), 1)
+    g.wait_ge(S("c0"), 1)
+    g.wait_ge(S("c1"), 1)
+    fused([tr(peers, off, "ua%d" % ci, own_u, [own_u for _k in peers])])
+
+    def own_u_ready():
+        Te.wait_ge(S("c0"), 1)
+        Te.wait_ge(S("c1"), 1)
+
+    mm_pass(T.UB, (T.PV0, T.PV1), ("pv0", "pv1", "ua"), own_u_ready)
+
+    for s, c in enumerate(order):
+        if s == 0:
+            Sc.wait_ge(S("c0"), 1)
+            Sc.wait_ge(S("c1"), 1)
+        else:
+            Sc.wait_ge(S("ua%d" % c), n_off)
+        Sc.activation(out=T.SQ[:, PW * s:PW * s + PW], in_=T.UB[:, PW * c:PW * c + PW],
+                      func=ActivationFunctionType.Square).then_inc(S("sq%d" % s), 1)
+    V.wait_ge(S("sq0"), 1)
+    for s in range(1, nch):
+        V.wait_ge(S("sq%d" % s), 1)
+        if s > 1:
+            V.wait_ge(S("ac%d" % (s - 1)), 1)
+        V.tensor_tensor(out=T.ACC[:], in0=(T.SQ[:, 0:PW] if s == 1 else T.ACC[:]), in1=T.SQ[:, PW * s:PW * s + PW],
+                        op=add).then_inc(S("ac%d" % s), 1)
+
+    V.wait_ge(S("c0"), 1)
+    V.wait_ge(S("c1"), 1)
+    for h, pv in enumerate((T.PV0, T.PV1)):
+        Sc.wait_ge(S("pv%d" % h), 1)
+        Sc.activation(out=T.Z[:, PW * h:PW * h + BW], in_=pv[:, 0:BW],
+                      func=ActivationFunctionType.Square).then_inc(S("zs%d" % h), 1)
+        V.wait_ge(S("zs%d" % h), 1)
+        V.tensor_tensor(out=T.Z[:, PW * h + BW:PW * h + PW], in0=pv[:, 0:BW],
+                        in1=T.UB[:, o + BW * h:o + BW * h + BW], op=mult).then_inc(S("zv%d" % h), 1)
+    Te.wait_ge(S("m1"), 1)
+    for h in range(2):
+        Te.wait_ge(S("zs%d" % h), 1)
+        Te.wait_ge(S("zv%d" % h), 1)
+        ins = Te.matmul(out=T.PP[:, 0:1], lhsT=T.Z[:, PW * h:PW * h + PW], rhs=T.ONES[:, 0:1],
+                        start=(h == 0), stop=(h == 1))
+    ins.then_inc(S("pp"), 1)
+    V.wait_ge(S("pp"), 1)
+    V.tensor_copy(T.LO[:, 0:1], T.PP[:, 0:1]).then_inc(S("lo"), 1)
+    g.wait_ge(S("lo"), 1)
+    fused([tr(peers, off, "pq", T.LO[:, 0:1], [T.L[:, s - 1:s] for s in range(1, nch)])])
+
+    Te.wait_ge(S("ac%d" % (nch - 1)), 1)
+    Te.matmul(out=T.PS[:, 0:BW], lhsT=T.ONES[:], rhs=T.ACC[:, 0:BW], start=True, stop=False)
+    Te.matmul(out=T.PS[:, 0:BW], lhsT=T.ONES[:], rhs=T.ACC[:, BW:PW], start=False, stop=True).then_inc(S("ps"), 1)
+    Te.matmul(out=T.PB[:, 0:BW], lhsT=T.ONES[:], rhs=T.ACC[:, 0:BW], start=True, stop=False)
+    Te.matmul(out=T.PB[:, 0:BW], lhsT=T.ONES[:], rhs=T.ACC[:, BW:PW], start=False, stop=False)
+    Sc.wait_ge(S("ps"), 1)
+    Sc.activation(out=T.N1[:], in_=T.PS[:, 0:BW], func=ActivationFunctionType.Sqrt).then_inc(S("n1"), 1)
+    V.wait_ge(S("n1"), 1)
+    V.reciprocal(T.D1[:], T.N1[:]).then_inc(S("d1"), 1)
+    V.wait_ge(S("d1"), 1)
+    V.wait_ge(S("e1"), 1)
+    V.wait_ge(S("e2"), 1)
+    V.tensor_tensor(out=T.DSQ[:], in0=T.D1[:], in1=T.D1[:], op=mult).then_inc(S("dsq"), 1)
+    V.tensor_tensor(out=T.E3C[BW:128, :], in0=T.E3B[BW:128, :], in1=T.D1[BW:128, :], op=mult).then_inc(S("eb"), 1)
+    V.wait_ge(S("dsq"), 1)
+    V.tensor_tensor(out=T.E3C[0:BW, :], in0=T.E3A[0:BW, :], in1=T.DSQ[0:BW, :], op=mult).then_inc(S("et"), 1)
+    V.wait_ge(S("eb"), 1)
+    V.wait_ge(S("et"), 1)
+    V.wait_ge(S("lo"), 1)
+    V.tensor_scalar(out=T.RHO[:], in0=T.E3C[:], scalar1=T.LO[:, 0:1], scalar2=None, op0=mult).then_inc(S("rho"), 1)
+    Te.wait_ge(S("rho"), 1)
+    Te.matmul(out=T.PB[:, 0:BW], lhsT=T.ONES[:], rhs=T.RHO[:], start=False, stop=False)
+    for h, pv in enumerate((T.PV0, T.PV1)):
+        V.tensor_tensor(out=T.TW[:, BW * h:BW * h + BW], in0=pv[:, 0:BW], in1=T.D1[:],
+                        op=mult).then_inc(S("tw%d" % h), 1)
+    V.wait_ge(S("tw0"), 1)
+    V.wait_ge(S("tw1"), 1)
+    V.tensor_tensor(out=T.W[:], in0=T.TW[:], in1=own_u, op=add).then_inc(S("w"), 1)
+
+    V.wait_ge(S("pq"), n_off * (nch - 1))
+    V.tensor_reduce(out=T.SR[:, 0:1], in_=T.L[:, 0:nch - 1], axis=AxisListType.X, op=add).then_inc(S("sr"), 1)
+    V.wait_ge(S("sr"), 1)
+    V.tensor_scalar(out=T.RHR[:], in0=T.E3C[:], scalar1=T.SR[:, 0:1], scalar2=None, op0=mult).then_inc(S("rhr"), 1)
+    Te.wait_ge(S("rhr"), 1)
+    Te.matmul(out=T.PB[:, 0:BW], lhsT=T.ONES[:], rhs=T.RHR[:], start=False, stop=True).then_inc(S("pb"), 1)
+    Sc.wait_ge(S("pb"), 1)
+    Sc.activation(out=T.N2[:], in_=T.PB[:, 0:BW], func=ActivationFunctionType.Sqrt).then_inc(S("n2"), 1)
+    V.wait_ge(S("n2"), 1)
+    V.reciprocal(T.PT[:, 0:BW], T.N2[:]).then_inc(S("d2"), 1)
+    V.wait_ge(S("d2"), 1)
+    V.wait_ge(S("w"), 1)
+    hs = sorted(range(2), key=lambda h: rc[h] == core)
+    for h in hs:
+        V.tensor_tensor(out=T.PT[:, BW * (h + 1):BW * (h + 2)], in0=T.W[:, BW * h:BW * h + BW], in1=T.PT[:, 0:BW],
+                        op=mult).then_inc(S("t%d" % h), 1)
+    V.wait_ge(S("xs"), xs_total)
+    for h in hs:
+        V.wait_ge(S("t%d" % h), 1)
+        out = T.YF[:, BW * b:BW * b + BW] if rc[h] == core else T.YS[:, BW * h:BW * h + BW]
+        V.tensor_tensor(out=out, in0=T.PT[:, BW * (h + 1):BW * (h + 2)],
+                        in1=T.XB[:, o + BW * h:o + BW * h + BW], op=add).then_inc(S("y%d" % h), 1)
+
+    h8 = n_on // 2
+    trs = []
+    for h in hs:
+        if rc[h] != core:
+            g.wait_ge(S("y%d" % h), 1)
+            trs.append(tr([rc[h]], _mk(onb[h8 * h:h8 * (h + 1)]), "ya", T.YS[:, BW * h:BW * h + BW],
+                          [T.YF[:, BW * b:BW * b + BW]]))
+    fused(trs)
+    g.wait_ge(S("ls"), sent[0])
+    if me_h is not None:
+        g.sync.wait_ge(S("ya"), h8 * (len(wk[ci]) - 1))
+        g.sync.wait_ge(S("y%d" % me_h), 1)
+        g.sync.dma_start(T.y[:], T.YF[:]).then_inc(S("st"), 16)
+        g.sync.wait_ge(S("st"), 16)

@@ -2,17 +2,22 @@ from concourse.bass import DstId, RemoteDMATransfer
 from concourse.mybir import AluOpType, AxisListType, ActivationFunctionType
 
 _F = "float32"
+_H = "bfloat16"
 SCRATCH = {
     "A": ("sbuf", [128, 3072], _F),
+    "AH": ("sbuf", [128, 3072], _H),
+    "AL": ("sbuf", [128, 3072], _H),
+    "UH": ("sbuf", [128, 768], _H),
+    "UL": ("sbuf", [128, 768], _H),
     "XF": ("sbuf", [128, 256], _F),
     "XB": ("sbuf", [128, 768], _F),
     "UB": ("sbuf", [128, 768], _F),
     "SQ": ("sbuf", [128, 768], _F),
     "ACC": ("sbuf", [128, 128], _F),
+    "ACC2": ("sbuf", [128, 64], _F),
     "ONES": ("sbuf", [128, 128], _F),
-    "TWOS": ("sbuf", [128, 64], _F),
-    "E3A": ("sbuf", [128, 64], _F),
-    "E3B": ("sbuf", [128, 64], _F),
+    "CV": ("sbuf", [128, 16], _F),
+    "E3": ("sbuf", [128, 128], _F),
     "E3C": ("sbuf", [128, 64], _F),
     "Z": ("sbuf", [128, 256], _F),
     "LO": ("sbuf", [128, 4], _F),
@@ -33,10 +38,13 @@ SCRATCH = {
     "PS": ("psum", [128, 512], _F), "PP": ("psum", [128, 512], _F),
     "PB": ("psum", [128, 512], _F), "PT": ("psum", [128, 512], _F),
 }
-SEMAPHORES = (["m1", "m2", "e1", "e2", "xl", "xs", "L0", "L1", "pu0", "pu1", "c0", "c1", "pv0", "pv1",
+SEMAPHORES = (["m1", "m2", "e1", "cs", "af", "xl", "xs", "L0", "L1", "pu0", "pu1", "c0", "c1", "pv0", "pv1",
                "zs0", "zs1", "zv0", "zv1", "pp", "lo", "ps", "n1", "d1", "dsq", "eb", "et", "rho", "tw0", "tw1",
                "w", "pq", "sr", "rhr", "pb", "n2", "d2", "t0", "t1", "y0", "y1", "ya", "st", "ls"]
               + ["A%d%d" % (h, c) for h in range(2) for c in range(6)]
+              + ["ah%d%d" % (h, c) for h in range(2) for c in range(6)]
+              + ["al%d%d" % (h, c) for h in range(2) for c in range(6)]
+              + ["uh%d" % c for c in range(6)] + ["ul%d" % c for c in range(6)]
               + ["xa%d" % c for c in range(6)] + ["ua%d" % c for c in range(6)]
               + ["sq%d" % c for c in range(6)] + ["ac%d" % c for c in range(1, 6)])
 
@@ -74,6 +82,7 @@ def rank_program(g, core, T, topo):
     rc = [cores[r] for r in rk[ci]]
     idle = [k for k in on_chip[ci] if k not in wk[ci]]
     xs_of = [[k for k in idle if topo.die(k) == topo.die(rc[h])][:2] for h in range(2)]
+    far = [d for d in cores if topo.chip(d) != topo.chip(core)][0]
 
     def S(n):
         return T.sem[n]
@@ -105,44 +114,76 @@ def rank_program(g, core, T, topo):
         return (RemoteDMATransfer(dst_ids=[did(k) for k in dsts_cores], dma_engine_mask=mask, remote_sem=S(sem),
                                   srcs=[src], dsts=dsts, alu_op=0), len(_bits(mask)))
 
+    def all_mask(k, ds):
+        m = topo.mask(k, ds[0])
+        for d in ds:
+            m &= topo.mask(k, d)
+        return m
+
+    V, Sc, Te = g.vector, g.scalar, g.tensor
+    CW = 128 // len(on_chip[ci])
+
+    kk = on_chip[ci].index(core)
+    e3s = T.E3[:, CW * kk:CW * kk + CW]
+    V.memset(T.CV[:, 0:CW], 1.0 if CW * kk < BW else 2.0).then_inc(S("m2"), 1)
+    g.wait_ge(S("m2"), 1)
+    g.affine_select(e3s, T.CV[:, 0:CW], [[-1, CW]], AluOpType.is_equal, 0.0, -CW * kk, 1).then_inc(S("e1"), 1)
+    g.wait_ge(S("e1"), 1)
+    cto = [w for w in wk[ci] if w != core]
+    fused([tr(cto, all_mask(core, cto), "cs", e3s, [e3s for _w in cto])])
+
+    def pair(h, c):
+        return T.A[:, acol(h, c):acol(h, c) + 256]
+
+    def relays(h):
+        near = [w for w in wk[ci] if w != rc[h] and topo.die(w) == topo.die(rc[h])][0]
+        rl = xs_of[h] + [near]
+        mb = _bits(all_mask(rc[h], rl))
+        q_ = len(mb) // 4
+        return [(rl[0], mb[0:q_]), (rl[1], mb[q_:2 * q_]), (rl[2], mb[2 * q_:4 * q_])]
+
+    def fw(h, k):
+        to = [w for w in wk[ci] if w != rc[h] and w != k]
+        m = all_mask(k, to)
+        if k in wk[ci]:
+            m &= ~topo.mask(k, far)
+        return to, m
+
+    assert half == 3
+
+    def pass_on(h):
+        rl = relays(h)
+        i = [r[0] for r in rl].index(core)
+        to, m = fw(h, core)
+        for s in (i, i + half):
+            c = order[s]
+            g.wait_ge(S("A%d%d" % (h, c)), len(rl[i][1]))
+            fused([tr(to, m, "A%d%d" % (h, c), pair(h, c), [pair(h, c) for _w in to])])
+
     if core in idle:
         for h in range(2):
             if core in xs_of[h]:
-                k = xs_of[h].index(core)
-                to = [w for w in wk[ci] if w != rc[h]]
-                mask = topo.mask(core, to[0])
-                for w in to:
-                    mask &= topo.mask(core, w)
-                g.wait_ge(S("L%d" % k), len(_bits(topo.mask(rc[h], core))))
-                for s in range(k * half, (k + 1) * half):
-                    c = order[s]
-                    ap = T.A[:, acol(h, c):acol(h, c) + 256]
-                    fused([tr(to, mask, "A%d%d" % (h, c), ap, [ap for _w in to])])
-                g.wait_ge(S("ls"), sent[0])
+                pass_on(h)
+        g.wait_ge(S("ls"), sent[0])
         return
 
     b = wk[ci].index(core)
     me_h = rc.index(core) if core in rc else None
     peers = [wk[dst_at(ci, s)][b] for s in range(1, nch)]
-    off = topo.mask(core, peers[0])
-    for k in peers:
-        off &= topo.mask(core, k)
+    off = all_mask(core, peers)
     n_off = len(_bits(off))
     mates_here = [w for w in wk[ci] if w != core]
-    on = topo.mask(core, mates_here[0])
-    for k in mates_here:
-        on &= topo.mask(core, k)
+    on = all_mask(core, mates_here)
     onb = _bits(on)
     n_on = len(onb)
     o = PW * ci
     own_x = T.XB[:, o:o + PW]
     own_u = T.UB[:, o:o + PW]
-    V, Sc, Te = g.vector, g.scalar, g.tensor
-    mult, add = AluOpType.mult, AluOpType.add
+    mult, add, sub = AluOpType.mult, AluOpType.add, AluOpType.subtract
+    Copy, Square = ActivationFunctionType.Copy, ActivationFunctionType.Square
     q4 = n_on // 4
 
     V.memset(T.ONES[:], 1.0).then_inc(S("m1"), 1)
-    V.memset(T.TWOS[:], 2.0).then_inc(S("m2"), 1)
 
     q = ci // half
     hw = 256 * half
@@ -153,11 +194,6 @@ def rank_program(g, core, T, topo):
         g.sync.dma_start(T.A[:, a0:a0 + hw], T.a[:, hw * q:hw * q + hw]).then_inc(S("L0"), 16)
         Sc.dma_start(T.A[:, a1:a1 + hw], T.a[:, hw * (1 - q):hw * (1 - q) + hw]).then_inc(S("L1"), 16)
 
-    g.wait_ge(S("m1"), 1)
-    g.wait_ge(S("m2"), 1)
-    g.affine_select(T.E3A[:], T.ONES[:, 0:BW], [[-1, BW]], AluOpType.is_equal, 0.0, 0, 1).then_inc(S("e1"), 1)
-    g.affine_select(T.E3B[:], T.TWOS[:], [[-1, BW]], AluOpType.is_equal, 0.0, -BW, 1).then_inc(S("e2"), 1)
-
     xs_total = sum(q4 for h in range(2) if rc[h] != core) + (16 if me_h is not None else 0)
     if me_h is not None:
         g.wait_ge(S("xl"), 16)
@@ -167,82 +203,109 @@ def rank_program(g, core, T, topo):
             trs.append(tr([w], _mk(onb[q4 * (i + 1):q4 * (i + 2)]), "xs", T.XF[:, BW * bw_:BW * bw_ + BW],
                           [T.XB[:, o + BW * me_h:o + BW * me_h + BW]]))
         fused(trs)
-        for k, a_ in enumerate((a0, a1)):
+        for k in range(2):
             g.wait_ge(S("L%d" % k), 16)
-            x_ = xs_of[me_h][k]
-            rid, pid, _s = topo.addr(x_)
-            mk_ = topo.mask(core, x_)
-            g.remote_dma(out_ap=T.A[:, a_:a_ + hw], in_ap=T.A[:, a_:a_ + hw], remote_sem=S("L%d" % k),
-                         local_sem=S("ls"), pid=pid, routing_id=rid, dma_engine_mask=mk_)
-            sent[0] += len(_bits(mk_))
+            fused([tr([r[0]], _mk(r[1]), "A%d%d" % (me_h, order[half * k + i]), pair(me_h, order[half * k + i]),
+                      [pair(me_h, order[half * k + i])]) for i, r in enumerate(relays(me_h))])
 
     g.wait_ge(S("xs"), xs_total)
     fused([tr(peers, off, "xa%d" % ci, own_x, [own_x for _k in peers])])
+    if me_h is None:
+        pass_on([h for h in range(2) if topo.die(rc[h]) == topo.die(core)][0])
 
-    def a_wait(h, c, s):
+    def a_sem(h, c, s):
         if me_h == h:
-            Te.wait_ge(S("L%d" % (s // half)), 16)
+            return ("L%d" % (s // half), 16)
+        r = relays(h)[s % half]
+        return ("A%d%d" % (h, c), len(r[1]) if r[0] == core else len(_bits(fw(h, r[0])[1])))
+
+    pus = (T.PU0, T.PU1)
+    for s, c in enumerate(order):
+        if s == 0:
+            Te.wait_ge(S("xs"), xs_total)
         else:
-            Te.wait_ge(S("A%d%d" % (h, c)), n_on)
+            Te.wait_ge(S("xa%d" % c), n_off)
+        for h in range(2):
+            nm, cnt = a_sem(h, c, s)
+            Te.wait_ge(S(nm), cnt)
+            for jj in range(2):
+                ac_ = acol(h, c) + 128 * jj
+                ins = Te.matmul(out=pus[h][:, 0:BW], lhsT=T.A[:, ac_:ac_ + 128],
+                                rhs=T.XB[:, PW * c + BW * jj:PW * c + BW * jj + BW],
+                                start=(s == 0 and jj == 0), stop=(s == nch - 1 and jj == 1))
+            if s == nch - 1:
+                ins.then_inc(S("pu%d" % h), 1)
 
-    def mm_pass(buf, outs, done, first):
-        for s, c in enumerate(order):
-            if s == 0:
-                first()
-            else:
-                Te.wait_ge(S("%s%d" % (done[2], c)), n_off)
-            for h in range(2):
-                if done[2] == "xa":
-                    a_wait(h, c, s)
-                for jj in range(2):
-                    ac_ = acol(h, c) + 128 * jj
-                    ins = Te.matmul(out=outs[h][:, 0:BW], lhsT=T.A[:, ac_:ac_ + 128],
-                                    rhs=buf[:, PW * c + BW * jj:PW * c + BW * jj + BW],
-                                    start=(s == 0 and jj == 0), stop=(s == nch - 1 and jj == 1))
-                    if s == nch - 1 and jj == 1:
-                        ins.then_inc(S(done[h]), 1)
+    seq = [(s, c, h) for s, c in enumerate(order) for h in range(2)]
+    seq.sort(key=lambda e: e[2] != me_h)
+    for s, c, h in seq:
+        nm, cnt = a_sem(h, c, s)
+        k0 = acol(h, c)
+        Sc.wait_ge(S(nm), cnt)
+        Sc.activation(out=T.AH[:, k0:k0 + 256], in_=pair(h, c), func=Copy).then_inc(S("ah%d%d" % (h, c)), 1)
+        V.wait_ge(S(nm), cnt)
+        V.wait_ge(S("ah%d%d" % (h, c)), 1)
+        V.tensor_tensor(out=T.AL[:, k0:k0 + 256], in0=pair(h, c), in1=T.AH[:, k0:k0 + 256],
+                        op=sub).then_inc(S("al%d%d" % (h, c)), 1)
 
-    mm_pass(T.XB, (T.PU0, T.PU1), ("pu0", "pu1", "xa"), lambda: Te.wait_ge(S("xs"), xs_total))
-
-    for h, pu in enumerate((T.PU0, T.PU1)):
-        V.wait_ge(S("pu%d" % h), 1)
-        V.tensor_copy(T.UB[:, o + BW * h:o + BW * h + BW], pu[:, 0:BW]).then_inc(S("c%d" % h), 1)
+    for h in range(2):
+        Sc.wait_ge(S("pu%d" % h), 1)
+        Sc.activation(out=T.UB[:, o + BW * h:o + BW * h + BW], in_=pus[h][:, 0:BW], func=Copy).then_inc(S("c%d" % h), 1)
     g.wait_ge(S("c0"), 1)
     g.wait_ge(S("c1"), 1)
     fused([tr(peers, off, "ua%d" % ci, own_u, [own_u for _k in peers])])
 
-    def own_u_ready():
-        Te.wait_ge(S("c0"), 1)
-        Te.wait_ge(S("c1"), 1)
-
-    mm_pass(T.UB, (T.PV0, T.PV1), ("pv0", "pv1", "ua"), own_u_ready)
-
     for s, c in enumerate(order):
-        if s == 0:
-            Sc.wait_ge(S("c0"), 1)
-            Sc.wait_ge(S("c1"), 1)
-        else:
-            Sc.wait_ge(S("ua%d" % c), n_off)
-        Sc.activation(out=T.SQ[:, PW * s:PW * s + PW], in_=T.UB[:, PW * c:PW * c + PW],
-                      func=ActivationFunctionType.Square).then_inc(S("sq%d" % s), 1)
-    V.wait_ge(S("sq0"), 1)
-    for s in range(1, nch):
-        V.wait_ge(S("sq%d" % s), 1)
-        if s > 1:
-            V.wait_ge(S("ac%d" % (s - 1)), 1)
-        V.tensor_tensor(out=T.ACC[:], in0=(T.SQ[:, 0:PW] if s == 1 else T.ACC[:]), in1=T.SQ[:, PW * s:PW * s + PW],
-                        op=add).then_inc(S("ac%d" % s), 1)
+        for qu in (Sc, V):
+            if s == 0:
+                qu.wait_ge(S("c0"), 1)
+                qu.wait_ge(S("c1"), 1)
+            else:
+                qu.wait_ge(S("ua%d" % c), n_off)
+        ub, uh, ul = T.UB[:, PW * c:PW * c + PW], T.UH[:, PW * c:PW * c + PW], T.UL[:, PW * c:PW * c + PW]
+        Sc.activation(out=uh, in_=ub, func=Copy).then_inc(S("uh%d" % c), 1)
+        Sc.activation(out=T.SQ[:, PW * s:PW * s + PW], in_=ub, func=Square).then_inc(S("sq%d" % s), 1)
+        V.wait_ge(S("uh%d" % c), 1)
+        V.tensor_tensor(out=ul, in0=ub, in1=uh, op=sub).then_inc(S("ul%d" % c), 1)
+        if s >= 1:
+            V.wait_ge(S("sq%d" % s), 1)
+            V.wait_ge(S("sq0" if s == 1 else "ac%d" % (s - 1)), 1)
+            V.tensor_tensor(out=T.ACC[:], in0=(T.SQ[:, 0:PW] if s == 1 else T.ACC[:]),
+                            in1=T.SQ[:, PW * s:PW * s + PW], op=add).then_inc(S("ac%d" % s), 1)
 
-    V.wait_ge(S("c0"), 1)
-    V.wait_ge(S("c1"), 1)
-    for h, pv in enumerate((T.PV0, T.PV1)):
+    pvs = (T.PV0, T.PV1)
+    for s, c in enumerate(order):
+        Te.wait_ge(S("uh%d" % c), 1)
+        for part in range(2):
+            if part == 1:
+                Te.wait_ge(S("ul%d" % c), 1)
+            for h in range(2):
+                if part == 0:
+                    Te.wait_ge(S("ah%d%d" % (h, c)), 1)
+                    Te.wait_ge(S("al%d%d" % (h, c)), 1)
+                for jj in range(2):
+                    k0 = acol(h, c) + 128 * jj
+                    u0 = PW * c + BW * jj
+                    terms = ((T.AH, T.UH), (T.AL, T.UH)) if part == 0 else ((T.AH, T.UL),)
+                    for ti, (lh, rh) in enumerate(terms):
+                        ins = Te.matmul(out=pvs[h][:, 0:BW], lhsT=lh[:, k0:k0 + 128], rhs=rh[:, u0:u0 + BW],
+                                        start=(s == 0 and part == 0 and jj == 0 and ti == 0),
+                                        stop=(s == nch - 1 and part == 1 and jj == 1))
+                if s == nch - 1 and part == 1:
+                    ins.then_inc(S("pv%d" % h), 1)
+
+    V.wait_ge(S("ac%d" % (nch - 1)), 1)
+    V.tensor_tensor(out=T.ACC2[:], in0=T.ACC[:, 0:BW], in1=T.ACC[:, BW:PW], op=add).then_inc(S("af"), 1)
+    Te.wait_ge(S("m1"), 1)
+    Te.wait_ge(S("af"), 1)
+    Te.matmul(out=T.PS[:, 0:BW], lhsT=T.ONES[:], rhs=T.ACC2[:], start=True, stop=True).then_inc(S("ps"), 1)
+
+    for h, pv in enumerate(pvs):
         Sc.wait_ge(S("pv%d" % h), 1)
-        Sc.activation(out=T.Z[:, PW * h:PW * h + BW], in_=pv[:, 0:BW],
-                      func=ActivationFunctionType.Square).then_inc(S("zs%d" % h), 1)
+        Sc.activation(out=T.Z[:, PW * h:PW * h + BW], in_=pv[:, 0:BW], func=Square).then_inc(S("zs%d" % h), 1)
         V.wait_ge(S("zs%d" % h), 1)
         V.tensor_tensor(out=T.Z[:, PW * h + BW:PW * h + PW], in0=pv[:, 0:BW],
                         in1=T.UB[:, o + BW * h:o + BW * h + BW], op=mult).then_inc(S("zv%d" % h), 1)
-    Te.wait_ge(S("m1"), 1)
     for h in range(2):
         Te.wait_ge(S("zs%d" % h), 1)
         Te.wait_ge(S("zv%d" % h), 1)
@@ -254,29 +317,25 @@ def rank_program(g, core, T, topo):
     g.wait_ge(S("lo"), 1)
     fused([tr(peers, off, "pq", T.LO[:, 0:1], [T.L[:, s - 1:s] for s in range(1, nch)])])
 
-    Te.wait_ge(S("ac%d" % (nch - 1)), 1)
-    Te.matmul(out=T.PS[:, 0:BW], lhsT=T.ONES[:], rhs=T.ACC[:, 0:BW], start=True, stop=False)
-    Te.matmul(out=T.PS[:, 0:BW], lhsT=T.ONES[:], rhs=T.ACC[:, BW:PW], start=False, stop=True).then_inc(S("ps"), 1)
-    Te.matmul(out=T.PB[:, 0:BW], lhsT=T.ONES[:], rhs=T.ACC[:, 0:BW], start=True, stop=False)
-    Te.matmul(out=T.PB[:, 0:BW], lhsT=T.ONES[:], rhs=T.ACC[:, BW:PW], start=False, stop=False)
+    Te.matmul(out=T.PB[:, 0:BW], lhsT=T.ONES[:], rhs=T.ACC2[:], start=True, stop=False)
     Sc.wait_ge(S("ps"), 1)
     Sc.activation(out=T.N1[:], in_=T.PS[:, 0:BW], func=ActivationFunctionType.Sqrt).then_inc(S("n1"), 1)
     V.wait_ge(S("n1"), 1)
     V.reciprocal(T.D1[:], T.N1[:]).then_inc(S("d1"), 1)
     V.wait_ge(S("d1"), 1)
     V.wait_ge(S("e1"), 1)
-    V.wait_ge(S("e2"), 1)
+    V.wait_ge(S("cs"), n_on * (len(on_chip[ci]) - 1))
     V.tensor_tensor(out=T.DSQ[:], in0=T.D1[:], in1=T.D1[:], op=mult).then_inc(S("dsq"), 1)
-    V.tensor_tensor(out=T.E3C[BW:128, :], in0=T.E3B[BW:128, :], in1=T.D1[BW:128, :], op=mult).then_inc(S("eb"), 1)
+    V.tensor_tensor(out=T.E3C[BW:128, :], in0=T.E3[BW:128, BW:PW], in1=T.D1[BW:128, :], op=mult).then_inc(S("eb"), 1)
     V.wait_ge(S("dsq"), 1)
-    V.tensor_tensor(out=T.E3C[0:BW, :], in0=T.E3A[0:BW, :], in1=T.DSQ[0:BW, :], op=mult).then_inc(S("et"), 1)
+    V.tensor_tensor(out=T.E3C[0:BW, :], in0=T.E3[0:BW, 0:BW], in1=T.DSQ[0:BW, :], op=mult).then_inc(S("et"), 1)
     V.wait_ge(S("eb"), 1)
     V.wait_ge(S("et"), 1)
     V.wait_ge(S("lo"), 1)
     V.tensor_scalar(out=T.RHO[:], in0=T.E3C[:], scalar1=T.LO[:, 0:1], scalar2=None, op0=mult).then_inc(S("rho"), 1)
     Te.wait_ge(S("rho"), 1)
     Te.matmul(out=T.PB[:, 0:BW], lhsT=T.ONES[:], rhs=T.RHO[:], start=False, stop=False)
-    for h, pv in enumerate((T.PV0, T.PV1)):
+    for h, pv in enumerate(pvs):
         V.tensor_tensor(out=T.TW[:, BW * h:BW * h + BW], in0=pv[:, 0:BW], in1=T.D1[:],
                         op=mult).then_inc(S("tw%d" % h), 1)
     V.wait_ge(S("tw0"), 1)

from concourse.bass import DstId, RemoteDMATransfer
from concourse.mybir import AluOpType, AxisListType, ActivationFunctionType

_F = "float32"
_H = "bfloat16"
SCRATCH = {
    "A": ("sbuf", [128, 3072], _F),
    "AH": ("sbuf", [128, 3072], _H),
    "AL": ("sbuf", [128, 3072], _H),
    "UH": ("sbuf", [128, 768], _H),
    "UL": ("sbuf", [128, 768], _H),
    "XF": ("sbuf", [128, 256], _F),
    "XB": ("sbuf", [128, 768], _F),
    "UB": ("sbuf", [128, 768], _F),
    "SQ": ("sbuf", [128, 768], _F),
    "ACC": ("sbuf", [128, 128], _F),
    "ACC2": ("sbuf", [128, 64], _F),
    "ONES": ("sbuf", [128, 128], _F),
    "CV": ("sbuf", [128, 16], _F),
    "E3": ("sbuf", [128, 128], _F),
    "E3C": ("sbuf", [128, 64], _F),
    "Z": ("sbuf", [128, 256], _F),
    "LO": ("sbuf", [128, 4], _F),
    "L": ("sbuf", [128, 8], _F),
    "SR": ("sbuf", [128, 4], _F),
    "N1": ("sbuf", [128, 64], _F),
    "D1": ("sbuf", [128, 64], _F),
    "DSQ": ("sbuf", [128, 64], _F),
    "RHO": ("sbuf", [128, 64], _F),
    "RHR": ("sbuf", [128, 64], _F),
    "TW": ("sbuf", [128, 128], _F),
    "W": ("sbuf", [128, 128], _F),
    "N2": ("sbuf", [128, 64], _F),
    "YS": ("sbuf", [128, 128], _F),
    "YF": ("sbuf", [128, 256], _F),
    "PU0": ("psum", [128, 512], _F), "PU1": ("psum", [128, 512], _F),
    "PV0": ("psum", [128, 512], _F), "PV1": ("psum", [128, 512], _F),
    "PS": ("psum", [128, 512], _F), "PP": ("psum", [128, 512], _F),
    "PB": ("psum", [128, 512], _F), "PT": ("psum", [128, 512], _F),
}
SEMAPHORES = (["m1", "m2", "e1", "cs", "af", "xl", "xs", "L0", "L1", "pu0", "pu1", "c0", "c1", "pv0", "pv1",
               "zs0", "zs1", "zv0", "zv1", "pp", "lo", "ps", "n1", "d1", "dsq", "eb", "et", "rho", "tw0", "tw1",
               "w", "pq", "sr", "rhr", "pb", "n2", "d2", "t0", "t1", "y0", "y1", "ya", "st", "ls"]
              + ["A%d%d" % (h, c) for h in range(2) for c in range(6)]
              + ["ah%d%d" % (h, c) for h in range(2) for c in range(6)]
              + ["al%d%d" % (h, c) for h in range(2) for c in range(6)]
              + ["uh%d" % c for c in range(6)] + ["ul%d" % c for c in range(6)]
              + ["xa%d" % c for c in range(6)] + ["ua%d" % c for c in range(6)]
              + ["sq%d" % c for c in range(6)] + ["ac%d" % c for c in range(1, 6)])

BW = 64
PW = 2 * BW


def _bits(mask):
    return [i for i in range(16) if (mask >> i) & 1]


def _mk(bits):
    return sum(1 << i for i in bits)


def rank_program(g, core, T, topo):
    cores = list(T.cores)
    chips = []
    for c in cores:
        if topo.chip(c) not in chips:
            chips.append(topo.chip(c))
    if topo.chip(core) not in chips:
        return
    nch = len(chips)
    half = nch // 2
    ci = chips.index(topo.chip(core))
    rk = [[i for i, c in enumerate(cores) if topo.chip(c) == ch] for ch in chips]
    for c in range(nch):
        assert rk[c] == [2 * c, 2 * c + 1]
    every = range(topo.CORES_PER_CHIP * topo.CHIPS)
    on_chip = [[k for k in every if topo.chip(k) == ch] for ch in chips]
    wk = [[k for k in on_chip[c] if all(topo.may_write(k, d) for d in cores if d != k)] for c in range(nch)]
    for c in range(nch):
        assert len(wk[c]) * BW == 256
    rc = [cores[r] for r in rk[ci]]
    idle = [k for k in on_chip[ci] if k not in wk[ci]]
    xs_of = [[k for k in idle if topo.die(k) == topo.die(rc[h])][:2] for h in range(2)]
    far = [d for d in cores if topo.chip(d) != topo.chip(core)][0]

    def S(n):
        return T.sem[n]

    def did(k):
        rid, pid, _s = topo.addr(k)
        return DstId(rid=rid, pnc=pid)

    def src_at(cj, s):
        q_, l = divmod(cj, half)
        return (q_ if s < half else 1 - q_) * half + (l - s) % half

    def dst_at(cj, s):
        q_, l = divmod(cj, half)
        return (q_ if s < half else 1 - q_) * half + (l + s) % half

    def acol(h, c):
        return 128 * 2 * nch * h + 128 * rk[c][0]

    order = [src_at(ci, s) for s in range(nch)]
    sent = [0]

    def fused(trs):
        g.remote_dma_fused([m[0] for m in trs], local_sem=S("ls"))
        for m in trs:
            sent[0] += m[1]

    def tr(dsts_cores, mask, sem, src, dsts):
        return (RemoteDMATransfer(dst_ids=[did(k) for k in dsts_cores], dma_engine_mask=mask, remote_sem=S(sem),
                                  srcs=[src], dsts=dsts, alu_op=0), len(_bits(mask)))

    def all_mask(k, ds):
        m = topo.mask(k, ds[0])
        for d in ds:
            m &= topo.mask(k, d)
        return m

    V, Sc, Te = g.vector, g.scalar, g.tensor
    CW = 128 // len(on_chip[ci])

    kk = on_chip[ci].index(core)
    e3s = T.E3[:, CW * kk:CW * kk + CW]
    V.memset(T.CV[:, 0:CW], 1.0 if CW * kk < BW else 2.0).then_inc(S("m2"), 1)
    g.wait_ge(S("m2"), 1)
    g.affine_select(e3s, T.CV[:, 0:CW], [[-1, CW]], AluOpType.is_equal, 0.0, -CW * kk, 1).then_inc(S("e1"), 1)
    g.wait_ge(S("e1"), 1)
    cto = [w for w in wk[ci] if w != core]
    fused([tr(cto, all_mask(core, cto), "cs", e3s, [e3s for _w in cto])])

    def pair(h, c):
        return T.A[:, acol(h, c):acol(h, c) + 256]

    def relays(h):
        near = [w for w in wk[ci] if w != rc[h] and topo.die(w) == topo.die(rc[h])][0]
        rl = xs_of[h] + [near]
        mb = _bits(all_mask(rc[h], rl))
        q_ = len(mb) // 4
        return [(rl[0], mb[0:q_]), (rl[1], mb[q_:2 * q_]), (rl[2], mb[2 * q_:4 * q_])]

    def fw(h, k):
        to = [w for w in wk[ci] if w != rc[h] and w != k]
        m = all_mask(k, to)
        if k in wk[ci]:
            m &= ~topo.mask(k, far)
        return to, m

    assert half == 3

    def pass_on(h):
        rl = relays(h)
        i = [r[0] for r in rl].index(core)
        to, m = fw(h, core)
        for s in (i, i + half):
            c = order[s]
            g.wait_ge(S("A%d%d" % (h, c)), len(rl[i][1]))
            fused([tr(to, m, "A%d%d" % (h, c), pair(h, c), [pair(h, c) for _w in to])])

    if core in idle:
        for h in range(2):
            if core in xs_of[h]:
                pass_on(h)
        g.wait_ge(S("ls"), sent[0])
        return

    b = wk[ci].index(core)
    me_h = rc.index(core) if core in rc else None
    peers = [wk[dst_at(ci, s)][b] for s in range(1, nch)]
    off = all_mask(core, peers)
    n_off = len(_bits(off))
    mates_here = [w for w in wk[ci] if w != core]
    on = all_mask(core, mates_here)
    onb = _bits(on)
    n_on = len(onb)
    o = PW * ci
    own_x = T.XB[:, o:o + PW]
    own_u = T.UB[:, o:o + PW]
    mult, add, sub = AluOpType.mult, AluOpType.add, AluOpType.subtract
    Copy, Square = ActivationFunctionType.Copy, ActivationFunctionType.Square
    q4 = n_on // 4

    V.memset(T.ONES[:], 1.0).then_inc(S("m1"), 1)

    q = ci // half
    hw = 256 * half
    if me_h is not None:
        g.sync.dma_start(T.XF[:], T.x[:]).then_inc(S("xl"), 16)
        Sc.dma_start(T.XB[:, o + BW * me_h:o + BW * me_h + BW], T.x[:, BW * b:BW * b + BW]).then_inc(S("xs"), 16)
        a0, a1 = acol(me_h, q * half), acol(me_h, (1 - q) * half)
        g.sync.dma_start(T.A[:, a0:a0 + hw], T.a[:, hw * q:hw * q + hw]).then_inc(S("L0"), 16)
        Sc.dma_start(T.A[:, a1:a1 + hw], T.a[:, hw * (1 - q):hw * (1 - q) + hw]).then_inc(S("L1"), 16)

    xs_total = sum(q4 for h in range(2) if rc[h] != core) + (16 if me_h is not None else 0)
    if me_h is not None:
        g.wait_ge(S("xl"), 16)
        trs = []
        for i, w in enumerate(mates_here):
            bw_ = wk[ci].index(w)
            trs.append(tr([w], _mk(onb[q4 * (i + 1):q4 * (i + 2)]), "xs", T.XF[:, BW * bw_:BW * bw_ + BW],
                          [T.XB[:, o + BW * me_h:o + BW * me_h + BW]]))
        fused(trs)
        for k in range(2):
            g.wait_ge(S("L%d" % k), 16)
            fused([tr([r[0]], _mk(r[1]), "A%d%d" % (me_h, order[half * k + i]), pair(me_h, order[half * k + i]),
                      [pair(me_h, order[half * k + i])]) for i, r in enumerate(relays(me_h))])

    g.wait_ge(S("xs"), xs_total)
    fused([tr(peers, off, "xa%d" % ci, own_x, [own_x for _k in peers])])
    if me_h is None:
        pass_on([h for h in range(2) if topo.die(rc[h]) == topo.die(core)][0])

    def a_sem(h, c, s):
        if me_h == h:
            return ("L%d" % (s // half), 16)
        r = relays(h)[s % half]
        return ("A%d%d" % (h, c), len(r[1]) if r[0] == core else len(_bits(fw(h, r[0])[1])))

    pus = (T.PU0, T.PU1)
    for s, c in enumerate(order):
        if s == 0:
            Te.wait_ge(S("xs"), xs_total)
        else:
            Te.wait_ge(S("xa%d" % c), n_off)
        for h in range(2):
            nm, cnt = a_sem(h, c, s)
            Te.wait_ge(S(nm), cnt)
            for jj in range(2):
                ac_ = acol(h, c) + 128 * jj
                ins = Te.matmul(out=pus[h][:, 0:BW], lhsT=T.A[:, ac_:ac_ + 128],
                                rhs=T.XB[:, PW * c + BW * jj:PW * c + BW * jj + BW],
                                start=(s == 0 and jj == 0), stop=(s == nch - 1 and jj == 1))
            if s == nch - 1:
                ins.then_inc(S("pu%d" % h), 1)

    seq = [(s, c, h) for s, c in enumerate(order) for h in range(2)]
    seq.sort(key=lambda e: e[2] != me_h)
    for s, c, h in seq:
        nm, cnt = a_sem(h, c, s)
        k0 = acol(h, c)
        Sc.wait_ge(S(nm), cnt)
        Sc.activation(out=T.AH[:, k0:k0 + 256], in_=pair(h, c), func=Copy).then_inc(S("ah%d%d" % (h, c)), 1)
        V.wait_ge(S(nm), cnt)
        V.wait_ge(S("ah%d%d" % (h, c)), 1)
        V.tensor_tensor(out=T.AL[:, k0:k0 + 256], in0=pair(h, c), in1=T.AH[:, k0:k0 + 256],
                        op=sub).then_inc(S("al%d%d" % (h, c)), 1)

    for h in range(2):
        Sc.wait_ge(S("pu%d" % h), 1)
        Sc.activation(out=T.UB[:, o + BW * h:o + BW * h + BW], in_=pus[h][:, 0:BW], func=Copy).then_inc(S("c%d" % h), 1)
    g.wait_ge(S("c0"), 1)
    g.wait_ge(S("c1"), 1)
    fused([tr(peers, off, "ua%d" % ci, own_u, [own_u for _k in peers])])

    for s, c in enumerate(order):
        for qu in (Sc, V):
            if s == 0:
                qu.wait_ge(S("c0"), 1)
                qu.wait_ge(S("c1"), 1)
            else:
                qu.wait_ge(S("ua%d" % c), n_off)
        ub, uh, ul = T.UB[:, PW * c:PW * c + PW], T.UH[:, PW * c:PW * c + PW], T.UL[:, PW * c:PW * c + PW]
        Sc.activation(out=uh, in_=ub, func=Copy).then_inc(S("uh%d" % c), 1)
        Sc.activation(out=T.SQ[:, PW * s:PW * s + PW], in_=ub, func=Square).then_inc(S("sq%d" % s), 1)
        V.wait_ge(S("uh%d" % c), 1)
        V.tensor_tensor(out=ul, in0=ub, in1=uh, op=sub).then_inc(S("ul%d" % c), 1)
        if s >= 1:
            V.wait_ge(S("sq%d" % s), 1)
            V.wait_ge(S("sq0" if s == 1 else "ac%d" % (s - 1)), 1)
            V.tensor_tensor(out=T.ACC[:], in0=(T.SQ[:, 0:PW] if s == 1 else T.ACC[:]),
                            in1=T.SQ[:, PW * s:PW * s + PW], op=add).then_inc(S("ac%d" % s), 1)

    pvs = (T.PV0, T.PV1)
    for s, c in enumerate(order):
        Te.wait_ge(S("uh%d" % c), 1)
        for part in range(2):
            if part == 1:
                Te.wait_ge(S("ul%d" % c), 1)
            for h in range(2):
                if part == 0:
                    Te.wait_ge(S("ah%d%d" % (h, c)), 1)
                    Te.wait_ge(S("al%d%d" % (h, c)), 1)
                for jj in range(2):
                    k0 = acol(h, c) + 128 * jj
                    u0 = PW * c + BW * jj
                    terms = ((T.AH, T.UH), (T.AL, T.UH)) if part == 0 else ((T.AH, T.UL),)
                    for ti, (lh, rh) in enumerate(terms):
                        ins = Te.matmul(out=pvs[h][:, 0:BW], lhsT=lh[:, k0:k0 + 128], rhs=rh[:, u0:u0 + BW],
                                        start=(s == 0 and part == 0 and jj == 0 and ti == 0),
                                        stop=(s == nch - 1 and part == 1 and jj == 1))
                if s == nch - 1 and part == 1:
                    ins.then_inc(S("pv%d" % h), 1)

    V.wait_ge(S("ac%d" % (nch - 1)), 1)
    V.tensor_tensor(out=T.ACC2[:], in0=T.ACC[:, 0:BW], in1=T.ACC[:, BW:PW], op=add).then_inc(S("af"), 1)
    Te.wait_ge(S("m1"), 1)
    Te.wait_ge(S("af"), 1)
    Te.matmul(out=T.PS[:, 0:BW], lhsT=T.ONES[:], rhs=T.ACC2[:], start=True, stop=True).then_inc(S("ps"), 1)

    for h, pv in enumerate(pvs):
        Sc.wait_ge(S("pv%d" % h), 1)
        Sc.activation(out=T.Z[:, PW * h:PW * h + BW], in_=pv[:, 0:BW], func=Square).then_inc(S("zs%d" % h), 1)
        V.wait_ge(S("zs%d" % h), 1)
        V.tensor_tensor(out=T.Z[:, PW * h + BW:PW * h + PW], in0=pv[:, 0:BW],
                        in1=T.UB[:, o + BW * h:o + BW * h + BW], op=mult).then_inc(S("zv%d" % h), 1)
    for h in range(2):
        Te.wait_ge(S("zs%d" % h), 1)
        Te.wait_ge(S("zv%d" % h), 1)
        ins = Te.matmul(out=T.PP[:, 0:1], lhsT=T.Z[:, PW * h:PW * h + PW], rhs=T.ONES[:, 0:1],
                        start=(h == 0), stop=(h == 1))
    ins.then_inc(S("pp"), 1)
    V.wait_ge(S("pp"), 1)
    V.tensor_copy(T.LO[:, 0:1], T.PP[:, 0:1]).then_inc(S("lo"), 1)
    g.wait_ge(S("lo"), 1)
    fused([tr(peers, off, "pq", T.LO[:, 0:1], [T.L[:, s - 1:s] for s in range(1, nch)])])

    Te.matmul(out=T.PB[:, 0:BW], lhsT=T.ONES[:], rhs=T.ACC2[:], start=True, stop=False)
    Sc.wait_ge(S("ps"), 1)
    Sc.activation(out=T.N1[:], in_=T.PS[:, 0:BW], func=ActivationFunctionType.Sqrt).then_inc(S("n1"), 1)
    V.wait_ge(S("n1"), 1)
    V.reciprocal(T.D1[:], T.N1[:]).then_inc(S("d1"), 1)
    V.wait_ge(S("d1"), 1)
    V.wait_ge(S("e1"), 1)
    V.wait_ge(S("cs"), n_on * (len(on_chip[ci]) - 1))
    V.tensor_tensor(out=T.DSQ[:], in0=T.D1[:], in1=T.D1[:], op=mult).then_inc(S("dsq"), 1)
    V.tensor_tensor(out=T.E3C[BW:128, :], in0=T.E3[BW:128, BW:PW], in1=T.D1[BW:128, :], op=mult).then_inc(S("eb"), 1)
    V.wait_ge(S("dsq"), 1)
    V.tensor_tensor(out=T.E3C[0:BW, :], in0=T.E3[0:BW, 0:BW], in1=T.DSQ[0:BW, :], op=mult).then_inc(S("et"), 1)
    V.wait_ge(S("eb"), 1)
    V.wait_ge(S("et"), 1)
    V.wait_ge(S("lo"), 1)
    V.tensor_scalar(out=T.RHO[:], in0=T.E3C[:], scalar1=T.LO[:, 0:1], scalar2=None, op0=mult).then_inc(S("rho"), 1)
    Te.wait_ge(S("rho"), 1)
    Te.matmul(out=T.PB[:, 0:BW], lhsT=T.ONES[:], rhs=T.RHO[:], start=False, stop=False)
    for h, pv in enumerate(pvs):
        V.tensor_tensor(out=T.TW[:, BW * h:BW * h + BW], in0=pv[:, 0:BW], in1=T.D1[:],
                        op=mult).then_inc(S("tw%d" % h), 1)
    V.wait_ge(S("tw0"), 1)
    V.wait_ge(S("tw1"), 1)
    V.tensor_tensor(out=T.W[:], in0=T.TW[:], in1=own_u, op=add).then_inc(S("w"), 1)

    V.wait_ge(S("pq"), n_off * (nch - 1))
    V.tensor_reduce(out=T.SR[:, 0:1], in_=T.L[:, 0:nch - 1], axis=AxisListType.X, op=add).then_inc(S("sr"), 1)
    V.wait_ge(S("sr"), 1)
    V.tensor_scalar(out=T.RHR[:], in0=T.E3C[:], scalar1=T.SR[:, 0:1], scalar2=None, op0=mult).then_inc(S("rhr"), 1)
    Te.wait_ge(S("rhr"), 1)
    Te.matmul(out=T.PB[:, 0:BW], lhsT=T.ONES[:], rhs=T.RHR[:], start=False, stop=True).then_inc(S("pb"), 1)
    Sc.wait_ge(S("pb"), 1)
    Sc.activation(out=T.N2[:], in_=T.PB[:, 0:BW], func=ActivationFunctionType.Sqrt).then_inc(S("n2"), 1)
    V.wait_ge(S("n2"), 1)
    V.reciprocal(T.PT[:, 0:BW], T.N2[:]).then_inc(S("d2"), 1)
    V.wait_ge(S("d2"), 1)
    V.wait_ge(S("w"), 1)
    hs = sorted(range(2), key=lambda h: rc[h] == core)
    for h in hs:
        V.tensor_tensor(out=T.PT[:, BW * (h + 1):BW * (h + 2)], in0=T.W[:, BW * h:BW * h + BW], in1=T.PT[:, 0:BW],
                        op=mult).then_inc(S("t%d" % h), 1)
    V.wait_ge(S("xs"), xs_total)
    for h in hs:
        V.wait_ge(S("t%d" % h), 1)
        out = T.YF[:, BW * b:BW * b + BW] if rc[h] == core else T.YS[:, BW * h:BW * h + BW]
        V.tensor_tensor(out=out, in0=T.PT[:, BW * (h + 1):BW * (h + 2)],
                        in1=T.XB[:, o + BW * h:o + BW * h + BW], op=add).then_inc(S("y%d" % h), 1)

    h8 = n_on // 2
    trs = []
    for h in hs:
        if rc[h] != core:
            g.wait_ge(S("y%d" % h), 1)
            trs.append(tr([rc[h]], _mk(onb[h8 * h:h8 * (h + 1)]), "ya", T.YS[:, BW * h:BW * h + BW],
                          [T.YF[:, BW * b:BW * b + BW]]))
    fused(trs)
    g.wait_ge(S("ls"), sent[0])
    if me_h is not None:
        g.sync.wait_ge(S("ya"), h8 * (len(wk[ci]) - 1))
        g.sync.wait_ge(S("y%d" % me_h), 1)
        g.sync.dma_start(T.y[:], T.YF[:]).then_inc(S("st"), 16)
        g.sync.wait_ge(S("st"), 16)
